import numpy as np
import ml_dtypes


def mxq(x, axis, fmt="e4m3"):
    dtype, down = {"e4m3": (ml_dtypes.float8_e4m3fn, 7), "e5m2": (ml_dtypes.float8_e5m2, 14)}[fmt]
    v = np.moveaxis(np.asarray(x, np.float32).astype(ml_dtypes.bfloat16).astype(np.float64), axis, -1)
    blocks = v.reshape(v.shape[:-1] + (-1, 32))
    amax = np.abs(blocks).max(-1, keepdims=True)
    byte = np.maximum(np.where(amax > 0, np.frexp(amax)[1] - 1 + 127, 0) - down, 1)
    scale = np.exp2(byte - 127.0)
    codes = (blocks / scale).astype(np.float32).astype(dtype).astype(np.float64)
    return np.moveaxis((codes * scale).reshape(v.shape), -1, axis)


WIDE = False


def mx_kscale(k):
    if not WIDE:
        return np.ones(k)
    levels = np.array([10, -10, 5, -5, 0])
    if k % 512:
        return np.exp2(np.random.permutation(np.resize(levels, k // 32))).repeat(32)
    a = np.empty((k // 512, 16))
    for p in range(k // 512):
        a[p, :8] = np.random.permutation(np.resize(levels, 8))
        for g in range(8):
            far = levels[np.abs(levels - a[p, g]) >= 10]
            a[p, g + 8] = far[np.random.randint(len(far))]
    return np.exp2(a.ravel()).repeat(32)


def f64(x):
    return np.asarray(x).astype(np.float64)


def striped(idx):
    return np.tile(idx.reshape(-1, 16).T, (8, 1)).astype(np.uint16)


def unstriped(offs):
    return offs[:16].T.reshape(-1).astype(np.int64)


def striped8(idx):
    return np.concatenate([x.reshape(-1, 16).T for x in idx]).astype(np.uint16)


def runs(offs, k):
    lists = np.stack([offs[16 * r : 16 * r + 16].T.reshape(-1) for r in range(8)]).astype(np.int64)
    return lists[np.arange(k) % 512 // 64]


def pack_weight(w):
    k, n = w.shape
    w = f64(np.asarray(w, np.float32).astype(ml_dtypes.bfloat16)).reshape(k // 32, 32, n)
    amax = np.abs(w).max(1)
    byte = np.clip(np.where(amax > 0, np.frexp(amax)[1] - 1 + 127 - 7, 1), 1, 254)
    scaled = (w * np.exp2(127.0 - byte)[:, None, :]).reshape(k, n).astype(np.float32)
    words = np.ascontiguousarray(scaled.reshape(k // 512, 128, 4, n).transpose(0, 1, 3, 2)).astype(ml_dtypes.float8_e4m3fn).view(np.uint8)
    return words, np.ascontiguousarray(byte.astype(np.uint8).reshape(k // 512, 16, n))


def unpack_weight(words, scales):
    g, p, n, _ = words.shape
    vals = np.ascontiguousarray(words).view(ml_dtypes.float8_e4m3fn).astype(np.float64) * np.repeat(np.exp2(scales.astype(np.float64) - 127.0), 8, axis=1)[..., None]
    return vals.transpose(0, 1, 3, 2).reshape(g * 512, n)


E2M1 = np.array([0.0, 0.5, 1.0, 1.5, 2.0, 3.0, 4.0, 6.0, -0.0, -0.5, -1.0, -1.5, -2.0, -3.0, -4.0, -6.0])


def pack_fp4(w):
    k, n = w.shape
    w = f64(np.asarray(w, np.float32).astype(ml_dtypes.bfloat16)).reshape(k // 32, 32, n)
    amax = np.abs(w).max(1)
    mant, ex = np.frexp(amax / 6.0)
    byte = np.clip(np.where(amax > 0, np.where(mant > 0.5, ex, ex - 1) + 127, 1), 1, 254)
    scaled = (w * np.exp2(127.0 - byte)[:, None, :]).reshape(k, n).astype(np.float32)
    c = np.ascontiguousarray(scaled.reshape(k // 512, 128, 4, n).transpose(0, 1, 3, 2)).astype(ml_dtypes.float4_e2m1fn).view(np.uint8) & 0xF
    words = (c[..., 0::2] | (c[..., 1::2] << 4)).reshape(k // 512, 128, 2 * n)
    return np.ascontiguousarray(words), np.ascontiguousarray(byte.astype(np.uint8).reshape(k // 512, 16, n))


def unpack_fp4(words, scales):
    g, _, n = scales.shape
    words = np.ascontiguousarray(words).reshape(g, 128, n, 2)
    nib = np.empty((g, 128, n, 4), np.uint8)
    nib[..., 0::2] = words & 0xF
    nib[..., 1::2] = words >> 4
    vals = E2M1[nib] * np.repeat(np.exp2(scales.astype(np.float64) - 127.0), 8, axis=1)[..., None]
    return vals.transpose(0, 1, 3, 2).reshape(g * 512, n)


def planes(y):
    n, m = y.shape
    v = y.astype(np.float32).astype(ml_dtypes.bfloat16).astype(np.float64).reshape(n // 32, 32, m)
    top = np.abs(v).max(1)
    byte = np.clip(np.where(top > 0, np.frexp(top)[1] - 1 + 127 - 7, 1), 1, 254)
    codes = (v * np.exp2(127.0 - byte)[:, None, :]).reshape(n, m).astype(np.float32).astype(ml_dtypes.float8_e4m3fn).view(np.uint8)
    words = codes.reshape(n // 512, 128, 4, m).transpose(0, 1, 3, 2)
    return np.ascontiguousarray(words), np.ascontiguousarray(byte.astype(np.uint8).reshape(n // 512, 16, m))


K, T, S, N, H = 512, 2048, 512, 512, 512


def setup_inputs():
    n = np.random.standard_normal
    s = mx_kscale(K)[:, None]
    u = mx_kscale(H)
    packed_xT = pack_weight(n((K, T)) * s)
    packed_w1 = pack_fp4(n((K, H)) / np.sqrt(K) / s)
    packed_w2 = pack_fp4(n((K, H)) / np.sqrt(K) / s)
    packed_w3 = pack_fp4(n((H, N)) / np.sqrt(H) / u[:, None])
    return {
        "x_words": packed_xT[0],
        "x_scales": packed_xT[1],
        "w1_words": packed_w1[0],
        "w1_scales": packed_w1[1],
        "w2_words": packed_w2[0],
        "w2_scales": packed_w2[1],
        "gn": (np.random.uniform(0.5, 1.5, (H, 1)) * u[:, None]).astype(np.float32),
        "w3_words": packed_w3[0],
        "w3_scales": packed_w3[1],
        "res": (2 * n((N, S))).astype(np.float32),
        "offs": striped(np.random.permutation(T)[:S]),
        "two": striped(np.random.permutation(T)[:S]),
        "hi": striped8(np.stack([np.random.permutation(S) for _ in range(8)])),
        "lo": striped8(np.stack([np.random.permutation(S) for _ in range(8)])),
    }


def reference(x_words, x_scales, w1_words, w1_scales, w2_words, w2_scales, gn, w3_words, w3_scales, res, offs, two, hi, lo):
    xq = unpack_weight(x_words, x_scales)[:, unstriped(offs)]
    y = unpack_fp4(w1_words, w1_scales).T @ xq
    dx = y[np.arange(H)[:, None], runs(hi, H)] - (y[np.arange(H)[:, None], runs(lo, H)])
    x_two = unpack_weight(x_words, x_scales)[:, unstriped(two)]
    c = unpack_fp4(w2_words, w2_scales).T @ x_two
    dy = c[np.arange(H)[:, None], runs(hi, H)] - (c[np.arange(H)[:, None], runs(lo, H)])
    z = f64(gn) * ((dx * dy) / ((dx) ** 2 + 0.25))
    out_0 = f64(res) + (unpack_fp4(w3_words, w3_scales).T @ mxq(z, 0, "e4m3"))
    return (out_0,) + planes(out_0)

@@ -1,0 +1,196 @@
+from contextlib import ExitStack
+
+import concourse.mybir as mybir
+
+F32 = mybir.dt.float32
+BF16 = mybir.dt.bfloat16
+I32 = mybir.dt.int32
+U32 = mybir.dt.uint32
+U16 = mybir.dt.uint16
+U8 = mybir.dt.uint8
+FP8X4 = mybir.dt.float8_e4m3fn_x4
+FP4X4 = mybir.dt.float4_e2m1fn_x4
+ACT = mybir.ActivationFunctionType
+ALU = mybir.AluOpType
+
+P = 128
+T = 2048
+S = 512
+H = 512
+PACK = 4
+HALF = 256
+CHUNK = 128
+FLOPS = 3 * 2 * 512 * 512 * 512
+
+
+def tile_picked_localslope_none_po_kernel(
+    tc, x_words, x_scales, w1_words, w1_scales, w2_words, w2_scales, gn, w3_words, w3_scales, res, offs, two, hi, lo, out_0, out_1, out_2
+):
+    nc = tc.nc
+    with ExitStack() as ctx:
+        lists = ctx.enter_context(tc.tile_pool(name="lists", bufs=1))
+        keep = ctx.enter_context(tc.tile_pool(name="keep", bufs=1))
+        psum = ctx.enter_context(tc.psum_pool(name="psum", bufs=1))
+
+        def load_scale_rows(queues, plane, rows):
+            for q in range(4):
+                queues[q].dma_start(plane[32 * q : 32 * q + 4, :].bitcast(I32), rows[4 * q : 4 * q + 4, :].bitcast(I32))
+
+        xs = keep.tile([P, T], U8, name="xs", align_bytes=64)
+        nc.gpsimd.memset(xs[:].bitcast(I32), 0)
+        ws_raw = keep.tile([P, 2 * H], U8, name="ws_raw", align_bytes=64)
+        nc.vector.memset(ws_raw[:].bitcast(I32), 0)
+        warm = keep.tile([P, 2], F32, name="warm")
+        nc.vector.memset(warm[:, 0:1], 1.0)
+
+        offs_sb = lists.tile([P, S // 16], U16, name="offs_sb")
+        two_sb = lists.tile([P, S // 16], U16, name="two_sb")
+        lo_sb = lists.tile([P, S // 16], U16, name="lo_sb")
+        hi_sb = lists.tile([P, S // 16], U16, name="hi_sb")
+        xw = keep.tile([P, T], I32, name="xw", tag="big", align_bytes=64)
+        w1_raw = keep.tile([P, 2 * H], U8, name="w1_raw", tag="w13", align_bytes=64)
+        w2_raw = keep.tile([P, 2 * H], U8, name="w2_raw", align_bytes=64)
+        sq = keep.tile([P, PACK * S], F32, name="sq")
+        gn_sb = sq[:, 0:PACK]
+        on_sync = [nc.sync] * 4
+
+        x_rows = x_words[0].rearrange("p c r -> p (c r)").bitcast(I32)
+        nc.sync.dma_start(offs_sb[:], offs)
+        nc.scalar.dma_start(xw[:, 0 : T // 2], x_rows[:, 0 : T // 2])
+        nc.sync.dma_start(two_sb[:], two)
+        load_scale_rows([nc.sync, nc.scalar, nc.sync, nc.scalar], xs, x_scales[0])
+        nc.scalar.dma_start(xw[:, T // 2 : T], x_rows[:, T // 2 : T])
+        nc.scalar.activation(warm[:, 1:2], warm[:, 0:1], ACT.Abs_reciprocal_sqrt)
+        nc.sync.dma_start(w1_raw[:].bitcast(I32), w1_words[0].bitcast(I32))
+        load_scale_rows(on_sync, ws_raw[:, 0:H], w1_scales[0])
+        nc.sync.dma_start(lo_sb[:], lo)
+        nc.sync.dma_start(hi_sb[:], hi)
+        nc.sync.dma_start(w2_raw[:].bitcast(I32), w2_words[0].bitcast(I32))
+        load_scale_rows(on_sync, ws_raw[:, H : 2 * H], w2_scales[0])
+        nc.sync.dma_start(gn_sb, gn.rearrange("(p t) o -> p (t o)", t=PACK))
+
+        def deal(engine, name, raw_words, raw_scales):
+            words = keep.tile([P, 2 * H], U8, name=name + "_words", align_bytes=64)
+            scales = keep.tile([P, H], U8, name=name + "_scales", align_bytes=64)
+            engine.tensor_copy(words[:].rearrange("p (t m b) -> p t m b", t=PACK, b=2), raw_words.rearrange("p (m t b) -> p t m b", t=PACK, b=2))
+            engine.tensor_copy(scales[:].rearrange("p (t m) -> p t m", t=PACK), raw_scales.rearrange("p (m t) -> p t m", t=PACK))
+            return words, scales
+
+        def pick_scales(name, offsets):
+            scales = keep.tile([P, S], U8, name=name, align_bytes=64)
+            nc.vector.tensor_copy(scales[:], xs[:].indirect(offsets[:]))
+            return scales
+
+        def pick_words(name, offsets):
+            words = keep.tile([P, S], I32, name=name, align_bytes=64)
+            nc.vector.tensor_copy(words[:].bitcast(U32), xw[:].bitcast(U32).indirect(offsets[:]))
+            return words
+
+        def product(out, w, t, rhs_words, rhs_scales):
+            nc.tensor.matmul_mx(
+                out=out,
+                lhsT=w[0][:, 2 * P * t : 2 * P * (t + 1)].bitcast(FP4X4),
+                lhsT_scale=w[1][:, P * t : P * (t + 1)],
+                rhs=rhs_words.bitcast(FP8X4),
+                rhs_scale=rhs_scales,
+                start=True,
+                stop=True,
+            )
+
+        w1 = deal(nc.gpsimd, "w1", w1_raw[:], ws_raw[:, 0:H])
+        xa_scales = pick_scales("xa_scales", offs_sb)
+        xb_scales = pick_scales("xb_scales", two_sb)
+        xa = (pick_words("xa_words", offs_sb), xa_scales)
+        xb = (pick_words("xb_words", two_sb), xb_scales)
+        w2 = deal(nc.gpsimd, "w2", w2_raw[:], ws_raw[:, H : 2 * H])
+
+        w3_raw = keep.tile([P, 2 * H], U8, name="w3_raw", tag="w13", align_bytes=64)
+        nc.sync.dma_start(w3_raw[:].bitcast(I32), w3_words[0].bitcast(I32))
+        load_scale_rows(on_sync, ws_raw[:, 0:H], w3_scales[0])
+        w3 = deal(nc.gpsimd, "w3", w3_raw[:], ws_raw[:, 0:H])
+        res_sb = keep.tile([P, PACK, S], F32, name="res_sb", tag="big", align_bytes=64)
+        nc.sync.dma_start(res_sb[:], res.rearrange("(p t) s -> p t s", t=PACK))
+
+        y_sb = {}
+        c_sb = {}
+        for t in reversed(range(PACK)):
+            bank = psum.tile([P, S], F32, name=f"y_bank{t}", tag=f"bank{t}")
+            product(bank[:], w1, t, xa[0][:], xa[1][:])
+            y_t = keep.tile([P, S], F32, name=f"y{t}")
+            nc.scalar.copy(y_t[:], bank[:])
+            y_sb[t] = y_t
+        for t in reversed(range(PACK)):
+            bank = psum.tile([P, S], F32, name=f"c_bank{t}", tag=f"bank{PACK + t}")
+            product(bank[:], w2, t, xb[0][:], xb[1][:])
+            c_t = keep.tile([P, S], F32, name=f"c{t}")
+            nc.scalar.activation(c_t[:], bank[:], ACT.Copy, scale=gn_sb[:, t : t + 1])
+            c_sb[t] = c_t
+
+        def slot(ring, n, h=None):
+            if h is None:
+                return ring[:, n * S : (n + 1) * S]
+            return ring[:, n * S + h * HALF : n * S + (h + 1) * HALF]
+
+        def entries(offsets, h):
+            return offsets[:, h * HALF // 16 : (h + 1) * HALF // 16]
+
+        def fetch_lo(ring, windows):
+            for t in reversed(range(PACK)):
+                for h in range(S // HALF):
+                    nc.vector.tensor_copy(slot(ring, t + 1, h), windows[t][:].indirect(entries(lo_sb, h)))
+
+        def subtract_from_hi(ring, windows, t):
+            for h in range(S // HALF):
+                nc.vector.tensor_tensor(slot(ring, t, h), windows[t][:].indirect(entries(hi_sb, h)), slot(ring, t + 1, h), ALU.subtract)
+
+        y_ring = keep.tile([P, 2 * PACK * S], F32, name="y_ring")
+        c_ring = keep.tile([P, (PACK + 1) * S], F32, name="c_ring")
+        root = keep.tile([P, PACK * S], F32, name="root")
+        inv = keep.tile([P, PACK * S], F32, name="inv")
+        fetch_lo(y_ring, y_sb)
+        for t in range(PACK):
+            subtract_from_hi(y_ring, y_sb, t)
+            nc.scalar.activation(slot(sq, t), slot(y_ring, t), ACT.Square)
+            nc.scalar.activation(slot(root, t), slot(sq, t), ACT.Abs_reciprocal_sqrt, bias=0.25)
+            nc.scalar.activation(slot(inv, t), slot(root, t), ACT.Square)
+        fetch_lo(c_ring, c_sb)
+        for t in range(PACK):
+            nc.vector.tensor_tensor(slot(y_ring, PACK + t), slot(y_ring, t), slot(inv, t), ALU.mult)
+        for t in range(PACK):
+            subtract_from_hi(c_ring, c_sb, t)
+        slope = y_ring[:, PACK * S : 2 * PACK * S]
+        dy = c_ring[:, 0 : PACK * S]
+
+        def by_pairs(rows, j):
+            return rows.rearrange("p (t s) -> p t s", t=PACK)[:, :, j * CHUNK : (j + 1) * CHUNK].rearrange("p t (c i) -> p c t i", i=2)
+
+        def woven(tile):
+            return tile[:].rearrange("p (c i t) -> p c t i", i=2, t=PACK)
+
+        z_words = keep.tile([P, S], U32, name="z_words", align_bytes=64)
+        z_scales = keep.tile([P, S], U8, name="z_scales", align_bytes=64)
+        o_words = keep.tile([P, S], I32, name="o_words", align_bytes=64)
+        o_scales = keep.tile([P, S], U8, name="o_scales", align_bytes=64)
+        out_rows = out_0.rearrange("(p t) s -> p t s", t=PACK)
+        out_words = out_1[0].rearrange("p c r -> p (c r)").bitcast(I32)
+        banks = []
+        for j in range(S // CHUNK):
+            cols = slice(j * CHUNK, (j + 1) * CHUNK)
+            z = keep.tile([P, PACK * CHUNK], BF16, name=f"z{j}", align_bytes=64)
+            nc.vector.tensor_tensor(woven(z), by_pairs(slope, j), by_pairs(dy, j), ALU.mult)
+            nc.vector.quantize_mx(out=z_words[:, cols].bitcast(FP8X4), scales=z_scales[:, cols], in_=z[:])
+            bank = psum.tile([P, PACK, CHUNK], F32, name=f"o_bank{j}", tag=f"bank{j}")
+            for t in range(PACK):
+                product(bank[:, t, :], w3, t, z_words[:, cols], z_scales[:, cols])
+            banks.append(bank)
+        for j in range(S // CHUNK):
+            cols = slice(j * CHUNK, (j + 1) * CHUNK)
+            o = keep.tile([P, PACK, CHUNK], F32, name=f"o{j}")
+            nc.vector.tensor_tensor(o[:], banks[j][:], res_sb[:, :, cols], ALU.add)
+            nc.sync.dma_start(out_rows[:, :, cols], o[:])
+            ob = keep.tile([P, PACK * CHUNK], BF16, name=f"ob{j}", align_bytes=64)
+            nc.scalar.copy(woven(ob), o[:].rearrange("p t (c i) -> p c t i", i=2))
+            nc.vector.quantize_mx(out=o_words[:, cols].bitcast(FP8X4), scales=o_scales[:, cols], in_=ob[:])
+            nc.sync.dma_start(out_words[:, cols], o_words[:, cols])
+        for q in range(4):
+            nc.sync.dma_start(out_2[0][4 * q : 4 * q + 4, :].bitcast(I32), o_scales[32 * q : 32 * q + 4, :].bitcast(I32))

@@ -50,18 +50,17 @@ def tile_picked_localslope_none_po_kernel(
         xw = keep.tile([P, T], I32, name="xw", tag="big", align_bytes=64)
         w1_raw = keep.tile([P, 2 * H], U8, name="w1_raw", tag="w13", align_bytes=64)
         w2_raw = keep.tile([P, 2 * H], U8, name="w2_raw", align_bytes=64)
-        sq = keep.tile([P, PACK * S], F32, name="sq")
+        sq = keep.tile([P, S], F32, name="sq")
         gn_sb = sq[:, 0:PACK]
         on_sync = [nc.sync] * 4
 
         x_rows = x_words[0].rearrange("p c r -> p (c r)").bitcast(I32)
         nc.sync.dma_start(offs_sb[:], offs)
-        nc.scalar.dma_start(xw[:, 0 : T // 2], x_rows[:, 0 : T // 2])
-        nc.sync.dma_start(two_sb[:], two)
-        load_scale_rows([nc.sync, nc.scalar, nc.sync, nc.scalar], xs, x_scales[0])
-        nc.scalar.dma_start(xw[:, T // 2 : T], x_rows[:, T // 2 : T])
+        nc.scalar.dma_start(w1_raw[:].bitcast(I32), w1_words[0].bitcast(I32))
         nc.scalar.activation(warm[:, 1:2], warm[:, 0:1], ACT.Abs_reciprocal_sqrt)
-        nc.sync.dma_start(w1_raw[:].bitcast(I32), w1_words[0].bitcast(I32))
+        nc.sync.dma_start(two_sb[:], two)
+        load_scale_rows(on_sync, xs, x_scales[0])
+        nc.sync.dma_start(xw[:], x_rows)
         load_scale_rows(on_sync, ws_raw[:, 0:H], w1_scales[0])
         nc.sync.dma_start(lo_sb[:], lo)
         nc.sync.dma_start(hi_sb[:], hi)
@@ -145,17 +144,17 @@ def tile_picked_localslope_none_po_kernel(
 
         y_ring = keep.tile([P, 2 * PACK * S], F32, name="y_ring")
         c_ring = keep.tile([P, (PACK + 1) * S], F32, name="c_ring")
-        root = keep.tile([P, PACK * S], F32, name="root")
+        root = keep.tile([P, S], F32, name="root")
         inv = keep.tile([P, PACK * S], F32, name="inv")
         fetch_lo(y_ring, y_sb)
         for t in range(PACK):
             subtract_from_hi(y_ring, y_sb, t)
-            nc.scalar.activation(slot(sq, t), slot(y_ring, t), ACT.Square)
-            nc.scalar.activation(slot(root, t), slot(sq, t), ACT.Abs_reciprocal_sqrt, bias=0.25)
-            nc.scalar.activation(slot(inv, t), slot(root, t), ACT.Square)
+            nc.scalar.activation(sq[:], slot(y_ring, t), ACT.Square)
+            nc.scalar.activation(root[:], sq[:], ACT.Abs_reciprocal_sqrt, bias=0.25)
+            nc.scalar.activation(slot(inv, t), root[:], ACT.Square)
         fetch_lo(c_ring, c_sb)
         for t in range(PACK):
-            nc.vector.tensor_tensor(slot(y_ring, PACK + t), slot(y_ring, t), slot(inv, t), ALU.mult)
+            nc.gpsimd.tensor_tensor(slot(y_ring, PACK + t), slot(y_ring, t), slot(inv, t), ALU.mult)
         for t in range(PACK):
             subtract_from_hi(c_ring, c_sb, t)
         slope = y_ring[:, PACK * S : 2 * PACK * S]
@@ -193,4 +192,4 @@ def tile_picked_localslope_none_po_kernel(
             nc.vector.quantize_mx(out=o_words[:, cols].bitcast(FP8X4), scales=o_scales[:, cols], in_=ob[:])
             nc.sync.dma_start(out_words[:, cols], o_words[:, cols])
         for q in range(4):
-            nc.sync.dma_start(out_2[0][4 * q : 4 * q + 4, :].bitcast(I32), o_scales[32 * q : 32 * q + 4, :].bitcast(I32))
+            (nc.scalar if q % 2 == 0 else nc.sync).dma_start(out_2[0][4 * q : 4 * q + 4, :].bitcast(I32), o_scales[32 * q : 32 * q + 4, :].bitcast(I32))

@@ -20,6 +20,8 @@ H = 512
 PACK = 4
 HALF = 256
 CHUNK = 128
+Y_ORDER = (3, 2, 0, 1)
+C_ORDER = (3, 2, 1, 0)
 FLOPS = 3 * 2 * 512 * 512 * 512
 
 
@@ -50,8 +52,7 @@ def tile_picked_localslope_none_po_kernel(
         xw = keep.tile([P, T], I32, name="xw", tag="big", align_bytes=64)
         w1_raw = keep.tile([P, 2 * H], U8, name="w1_raw", tag="w13", align_bytes=64)
         w2_raw = keep.tile([P, 2 * H], U8, name="w2_raw", align_bytes=64)
-        sq = keep.tile([P, S], F32, name="sq")
-        gn_sb = sq[:, 0:PACK]
+        gn_sb = keep.tile([P, PACK], F32, name="gn_sb")
         on_sync = [nc.sync] * 4
 
         x_rows = x_words[0].rearrange("p c r -> p (c r)").bitcast(I32)
@@ -66,13 +67,13 @@ def tile_picked_localslope_none_po_kernel(
         nc.sync.dma_start(hi_sb[:], hi)
         nc.sync.dma_start(w2_raw[:].bitcast(I32), w2_words[0].bitcast(I32))
         load_scale_rows(on_sync, ws_raw[:, H : 2 * H], w2_scales[0])
-        nc.sync.dma_start(gn_sb, gn.rearrange("(p t) o -> p (t o)", t=PACK))
+        nc.sync.dma_start(gn_sb[:], gn.rearrange("(p t) o -> p (t o)", t=PACK))
 
-        def deal(engine, name, raw_words, raw_scales):
+        def deal(engine, scale_engine, name, raw_words, raw_scales):
             words = keep.tile([P, 2 * H], U8, name=name + "_words", align_bytes=64)
             scales = keep.tile([P, H], U8, name=name + "_scales", align_bytes=64)
             engine.tensor_copy(words[:].rearrange("p (t m b) -> p t m b", t=PACK, b=2), raw_words.rearrange("p (m t b) -> p t m b", t=PACK, b=2))
-            engine.tensor_copy(scales[:].rearrange("p (t m) -> p t m", t=PACK), raw_scales.rearrange("p (m t) -> p t m", t=PACK))
+            scale_engine.tensor_copy(scales[:].rearrange("p (t m) -> p t m", t=PACK), raw_scales.rearrange("p (m t) -> p t m", t=PACK))
             return words, scales
 
         def pick_scales(name, offsets):
@@ -96,23 +97,23 @@ def tile_picked_localslope_none_po_kernel(
                 stop=True,
             )
 
-        w1 = deal(nc.gpsimd, "w1", w1_raw[:], ws_raw[:, 0:H])
+        w1 = deal(nc.vector, nc.gpsimd, "w1", w1_raw[:], ws_raw[:, 0:H])
         xa_scales = pick_scales("xa_scales", offs_sb)
         xb_scales = pick_scales("xb_scales", two_sb)
         xa = (pick_words("xa_words", offs_sb), xa_scales)
         xb = (pick_words("xb_words", two_sb), xb_scales)
-        w2 = deal(nc.gpsimd, "w2", w2_raw[:], ws_raw[:, H : 2 * H])
+        w2 = deal(nc.gpsimd, nc.gpsimd, "w2", w2_raw[:], ws_raw[:, H : 2 * H])
 
         w3_raw = keep.tile([P, 2 * H], U8, name="w3_raw", tag="w13", align_bytes=64)
         nc.sync.dma_start(w3_raw[:].bitcast(I32), w3_words[0].bitcast(I32))
         load_scale_rows(on_sync, ws_raw[:, 0:H], w3_scales[0])
-        w3 = deal(nc.gpsimd, "w3", w3_raw[:], ws_raw[:, 0:H])
+        w3 = deal(nc.gpsimd, nc.gpsimd, "w3", w3_raw[:], ws_raw[:, 0:H])
         res_sb = keep.tile([P, PACK, S], F32, name="res_sb", tag="big", align_bytes=64)
         nc.sync.dma_start(res_sb[:], res.rearrange("(p t) s -> p t s", t=PACK))
 
         y_sb = {}
         c_sb = {}
-        for t in reversed(range(PACK)):
+        for t in Y_ORDER:
             bank = psum.tile([P, S], F32, name=f"y_bank{t}", tag=f"bank{t}")
             product(bank[:], w1, t, xa[0][:], xa[1][:])
             y_t = keep.tile([P, S], F32, name=f"y{t}")
@@ -133,31 +134,32 @@ def tile_picked_localslope_none_po_kernel(
         def entries(offsets, h):
             return offsets[:, h * HALF // 16 : (h + 1) * HALF // 16]
 
-        def fetch_lo(ring, windows):
-            for t in reversed(range(PACK)):
+        def fetch_lo(ring, ahead, windows, order):
+            for t in order:
                 for h in range(S // HALF):
-                    nc.vector.tensor_copy(slot(ring, t + 1, h), windows[t][:].indirect(entries(lo_sb, h)))
+                    nc.vector.tensor_copy(slot(ring, t + ahead, h), windows[t][:].indirect(entries(lo_sb, h)))
 
-        def subtract_from_hi(ring, windows, t):
+        def subtract_from_hi(ring, ahead, windows, t):
             for h in range(S // HALF):
-                nc.vector.tensor_tensor(slot(ring, t, h), windows[t][:].indirect(entries(hi_sb, h)), slot(ring, t + 1, h), ALU.subtract)
+                nc.vector.tensor_tensor(slot(ring, t, h), windows[t][:].indirect(entries(hi_sb, h)), slot(ring, t + ahead, h), ALU.subtract)
 
-        y_ring = keep.tile([P, 2 * PACK * S], F32, name="y_ring")
+        y_ring = keep.tile([P, (2 * PACK + 1) * S], F32, name="y_ring")
         c_ring = keep.tile([P, (PACK + 1) * S], F32, name="c_ring")
-        root = keep.tile([P, S], F32, name="root")
+        sq = [keep.tile([P, S], F32, name=f"sq{n}", tag=tag, align_bytes=64) for n, tag in enumerate(("xb_words", "w2_words"))]
+        root = keep.tile([P, 2 * S], F32, name="root")
         inv = keep.tile([P, PACK * S], F32, name="inv")
-        fetch_lo(y_ring, y_sb)
+        fetch_lo(y_ring, 2, y_sb, Y_ORDER)
         for t in range(PACK):
-            subtract_from_hi(y_ring, y_sb, t)
-            nc.scalar.activation(sq[:], slot(y_ring, t), ACT.Square)
-            nc.scalar.activation(root[:], sq[:], ACT.Abs_reciprocal_sqrt, bias=0.25)
-            nc.scalar.activation(slot(inv, t), root[:], ACT.Square)
-        fetch_lo(c_ring, c_sb)
+            subtract_from_hi(y_ring, 2, y_sb, t)
+            nc.scalar.activation(sq[t % 2][:], slot(y_ring, t), ACT.Square)
+            nc.scalar.activation(slot(root, t % 2), sq[t % 2][:], ACT.Abs_reciprocal_sqrt, bias=0.25)
+            nc.scalar.activation(slot(inv, t), slot(root, t % 2), ACT.Square)
+        fetch_lo(c_ring, 1, c_sb, C_ORDER)
         for t in range(PACK):
-            nc.gpsimd.tensor_tensor(slot(y_ring, PACK + t), slot(y_ring, t), slot(inv, t), ALU.mult)
+            (nc.gpsimd if t < PACK - 1 else nc.vector).tensor_tensor(slot(y_ring, PACK + 1 + t), slot(y_ring, t), slot(inv, t), ALU.mult)
         for t in range(PACK):
-            subtract_from_hi(c_ring, c_sb, t)
-        slope = y_ring[:, PACK * S : 2 * PACK * S]
+            subtract_from_hi(c_ring, 1, c_sb, t)
+        slope = y_ring[:, (PACK + 1) * S : (2 * PACK + 1) * S]
         dy = c_ring[:, 0 : PACK * S]
 
         def by_pairs(rows, j):

@@ -81,9 +81,11 @@ def tile_picked_localslope_none_po_kernel(
             nc.vector.tensor_copy(scales[:], xs[:].indirect(offsets[:]))
             return scales
 
-        def pick_words(name, offsets):
+        def pick_words(name, offsets, pieces):
             words = keep.tile([P, S], I32, name=name, align_bytes=64)
-            nc.vector.tensor_copy(words[:].bitcast(U32), xw[:].bitcast(U32).indirect(offsets[:]))
+            width = S // pieces
+            for h in range(pieces):
+                nc.vector.tensor_copy(words[:, h * width : (h + 1) * width].bitcast(U32), xw[:].bitcast(U32).indirect(offsets[:, h * width // 16 : (h + 1) * width // 16]))
             return words
 
         def product(out, w, t, rhs_words, rhs_scales):
@@ -100,8 +102,8 @@ def tile_picked_localslope_none_po_kernel(
         w1 = deal(nc.vector, nc.gpsimd, "w1", w1_raw[:], ws_raw[:, 0:H])
         xa_scales = pick_scales("xa_scales", offs_sb)
         xb_scales = pick_scales("xb_scales", two_sb)
-        xa = (pick_words("xa_words", offs_sb), xa_scales)
-        xb = (pick_words("xb_words", two_sb), xb_scales)
+        xa = (pick_words("xa_words", offs_sb, 2), xa_scales)
+        xb = (pick_words("xb_words", two_sb, 1), xb_scales)
         w2 = deal(nc.gpsimd, nc.gpsimd, "w2", w2_raw[:], ws_raw[:, H : 2 * H])
 
         w3_raw = keep.tile([P, 2 * H], U8, name="w3_raw", tag="w13", align_bytes=64)
@@ -114,6 +116,14 @@ def tile_picked_localslope_none_po_kernel(
         y_sb = {}
         c_sb = {}
         for t in Y_ORDER:
+            if t == Y_ORDER[0]:
+                y_sb[t] = keep.tile([P, S], F32, name=f"y{t}")
+                for h in range(2):
+                    cols = slice(h * HALF, (h + 1) * HALF)
+                    bank = psum.tile([P, HALF], F32, name=f"y_half{h}", tag=f"bank{t + PACK * h}")
+                    product(bank[:], w1, t, xa[0][:, cols], xa[1][:, cols])
+                    nc.scalar.copy(y_sb[t][:, cols], bank[:])
+                continue
             bank = psum.tile([P, S], F32, name=f"y_bank{t}", tag=f"bank{t}")
             product(bank[:], w1, t, xa[0][:], xa[1][:])
             y_t = keep.tile([P, S], F32, name=f"y{t}")
@@ -155,18 +165,20 @@ def tile_picked_localslope_none_po_kernel(
             nc.scalar.activation(slot(root, t % 2), sq[t % 2][:], ACT.Abs_reciprocal_sqrt, bias=0.25)
             nc.scalar.activation(slot(inv, t), slot(root, t % 2), ACT.Square)
         fetch_lo(c_ring, 1, c_sb, C_ORDER)
-        for t in range(PACK):
-            (nc.gpsimd if t < PACK - 1 else nc.vector).tensor_tensor(slot(y_ring, PACK + 1 + t), slot(y_ring, t), slot(inv, t), ALU.mult)
+        for t in range(PACK - 1):
+            nc.gpsimd.tensor_tensor(slot(y_ring, PACK + 1 + t), slot(y_ring, t), slot(inv, t), ALU.mult)
+        for h in range(2):
+            nc.vector.tensor_tensor(slot(y_ring, 2 * PACK, h), slot(y_ring, PACK - 1, h), slot(inv, PACK - 1, h), ALU.mult)
         for t in range(PACK):
             subtract_from_hi(c_ring, 1, c_sb, t)
         slope = y_ring[:, (PACK + 1) * S : (2 * PACK + 1) * S]
         dy = c_ring[:, 0 : PACK * S]
 
         def by_pairs(rows, j):
-            return rows.rearrange("p (t s) -> p t s", t=PACK)[:, :, j * CHUNK : (j + 1) * CHUNK].rearrange("p t (c i) -> p c t i", i=2)
+            return rows.rearrange("p (t s) -> p t s", t=PACK)[:, :, j * CHUNK : (j + 1) * CHUNK]
 
         def woven(tile):
-            return tile[:].rearrange("p (c i t) -> p c t i", i=2, t=PACK)
+            return tile[:].rearrange("p (c t) -> p c t", t=PACK)
 
         z_words = keep.tile([P, S], U32, name="z_words", align_bytes=64)
         z_scales = keep.tile([P, S], U8, name="z_scales", align_bytes=64)
@@ -178,7 +190,13 @@ def tile_picked_localslope_none_po_kernel(
         for j in range(S // CHUNK):
             cols = slice(j * CHUNK, (j + 1) * CHUNK)
             z = keep.tile([P, PACK * CHUNK], BF16, name=f"z{j}", align_bytes=64)
-            nc.vector.tensor_tensor(woven(z), by_pairs(slope, j), by_pairs(dy, j), ALU.mult)
+            if j < 2:
+                z_rows = keep.tile([P, PACK, CHUNK], BF16, name=f"z_rows{j}")
+                nc.vector.tensor_tensor(z_rows[:], by_pairs(slope, j), by_pairs(dy, j), ALU.mult)
+                nc.scalar.copy(woven(z), z_rows[:].rearrange("p t c -> p c t"))
+            else:
+                pairs = "p t (c i) -> p c t i"
+                nc.vector.tensor_tensor(z[:].rearrange("p (c i t) -> p c t i", i=2, t=PACK), by_pairs(slope, j).rearrange(pairs, i=2), by_pairs(dy, j).rearrange(pairs, i=2), ALU.mult)
             nc.vector.quantize_mx(out=z_words[:, cols].bitcast(FP8X4), scales=z_scales[:, cols], in_=z[:])
             bank = psum.tile([P, PACK, CHUNK], F32, name=f"o_bank{j}", tag=f"bank{j}")
             for t in range(PACK):
@@ -190,7 +208,7 @@ def tile_picked_localslope_none_po_kernel(
             nc.vector.tensor_tensor(o[:], banks[j][:], res_sb[:, :, cols], ALU.add)
             nc.sync.dma_start(out_rows[:, :, cols], o[:])
             ob = keep.tile([P, PACK * CHUNK], BF16, name=f"ob{j}", align_bytes=64)
-            nc.scalar.copy(woven(ob), o[:].rearrange("p t (c i) -> p c t i", i=2))
+            nc.scalar.copy(woven(ob), o[:].rearrange("p t c -> p c t"))
             nc.vector.quantize_mx(out=o_words[:, cols].bitcast(FP8X4), scales=o_scales[:, cols], in_=ob[:])
             nc.sync.dma_start(out_words[:, cols], o_words[:, cols])
         for q in range(4):

from contextlib import ExitStack

import concourse.mybir as mybir

F32 = mybir.dt.float32
BF16 = mybir.dt.bfloat16
I32 = mybir.dt.int32
U32 = mybir.dt.uint32
U16 = mybir.dt.uint16
U8 = mybir.dt.uint8
FP8X4 = mybir.dt.float8_e4m3fn_x4
FP4X4 = mybir.dt.float4_e2m1fn_x4
ACT = mybir.ActivationFunctionType
ALU = mybir.AluOpType

P = 128
T = 2048
S = 512
H = 512
PACK = 4
HALF = 256
CHUNK = 128
Y_ORDER = (3, 2, 0, 1)
C_ORDER = (3, 2, 1, 0)
FLOPS = 3 * 2 * 512 * 512 * 512


def tile_picked_localslope_none_po_kernel(
    tc, x_words, x_scales, w1_words, w1_scales, w2_words, w2_scales, gn, w3_words, w3_scales, res, offs, two, hi, lo, out_0, out_1, out_2
):
    nc = tc.nc
    with ExitStack() as ctx:
        lists = ctx.enter_context(tc.tile_pool(name="lists", bufs=1))
        keep = ctx.enter_context(tc.tile_pool(name="keep", bufs=1))
        psum = ctx.enter_context(tc.psum_pool(name="psum", bufs=1))

        def load_scale_rows(queues, plane, rows):
            for q in range(4):
                queues[q].dma_start(plane[32 * q : 32 * q + 4, :].bitcast(I32), rows[4 * q : 4 * q + 4, :].bitcast(I32))

        xs = keep.tile([P, T], U8, name="xs", align_bytes=64)
        nc.gpsimd.memset(xs[:].bitcast(I32), 0)
        ws_raw = keep.tile([P, 2 * H], U8, name="ws_raw", align_bytes=64)
        nc.vector.memset(ws_raw[:].bitcast(I32), 0)
        warm = keep.tile([P, 2], F32, name="warm")
        nc.vector.memset(warm[:, 0:1], 1.0)

        offs_sb = lists.tile([P, S // 16], U16, name="offs_sb")
        two_sb = lists.tile([P, S // 16], U16, name="two_sb")
        lo_sb = lists.tile([P, S // 16], U16, name="lo_sb")
        hi_sb = lists.tile([P, S // 16], U16, name="hi_sb")
        xw = keep.tile([P, T], I32, name="xw", tag="big", align_bytes=64)
        w1_raw = keep.tile([P, 2 * H], U8, name="w1_raw", tag="w13", align_bytes=64)
        w2_raw = keep.tile([P, 2 * H], U8, name="w2_raw", align_bytes=64)
        gn_sb = keep.tile([P, PACK], F32, name="gn_sb")
        on_sync = [nc.sync] * 4

        x_rows = x_words[0].rearrange("p c r -> p (c r)").bitcast(I32)
        nc.sync.dma_start(offs_sb[:], offs)
        nc.scalar.dma_start(w1_raw[:].bitcast(I32), w1_words[0].bitcast(I32))
        nc.scalar.activation(warm[:, 1:2], warm[:, 0:1], ACT.Abs_reciprocal_sqrt)
        nc.sync.dma_start(two_sb[:], two)
        load_scale_rows(on_sync, xs, x_scales[0])
        nc.sync.dma_start(xw[:], x_rows)
        load_scale_rows(on_sync, ws_raw[:, 0:H], w1_scales[0])
        nc.sync.dma_start(lo_sb[:], lo)
        nc.sync.dma_start(hi_sb[:], hi)
        nc.sync.dma_start(w2_raw[:].bitcast(I32), w2_words[0].bitcast(I32))
        load_scale_rows(on_sync, ws_raw[:, H : 2 * H], w2_scales[0])
        nc.sync.dma_start(gn_sb[:], gn.rearrange("(p t) o -> p (t o)", t=PACK))

        def deal(engine, scale_engine, name, raw_words, raw_scales):
            words = keep.tile([P, 2 * H], U8, name=name + "_words", align_bytes=64)
            scales = keep.tile([P, H], U8, name=name + "_scales", align_bytes=64)
            engine.tensor_copy(words[:].rearrange("p (t m b) -> p t m b", t=PACK, b=2), raw_words.rearrange("p (m t b) -> p t m b", t=PACK, b=2))
            scale_engine.tensor_copy(scales[:].rearrange("p (t m) -> p t m", t=PACK), raw_scales.rearrange("p (m t) -> p t m", t=PACK))
            return words, scales

        def pick_scales(name, offsets):
            scales = keep.tile([P, S], U8, name=name, align_bytes=64)
            nc.vector.tensor_copy(scales[:], xs[:].indirect(offsets[:]))
            return scales

        def pick_words(name, offsets, pieces):
            words = keep.tile([P, S], I32, name=name, align_bytes=64)
            width = S // pieces
            for h in range(pieces):
                nc.vector.tensor_copy(words[:, h * width : (h + 1) * width].bitcast(U32), xw[:].bitcast(U32).indirect(offsets[:, h * width // 16 : (h + 1) * width // 16]))
            return words

        def product(out, w, t, rhs_words, rhs_scales):
            nc.tensor.matmul_mx(
                out=out,
                lhsT=w[0][:, 2 * P * t : 2 * P * (t + 1)].bitcast(FP4X4),
                lhsT_scale=w[1][:, P * t : P * (t + 1)],
                rhs=rhs_words.bitcast(FP8X4),
                rhs_scale=rhs_scales,
                start=True,
                stop=True,
            )

        w1 = deal(nc.vector, nc.gpsimd, "w1", w1_raw[:], ws_raw[:, 0:H])
        xa_scales = pick_scales("xa_scales", offs_sb)
        xb_scales = pick_scales("xb_scales", two_sb)
        xa = (pick_words("xa_words", offs_sb, 2), xa_scales)
        xb = (pick_words("xb_words", two_sb, 1), xb_scales)
        w2 = deal(nc.gpsimd, nc.gpsimd, "w2", w2_raw[:], ws_raw[:, H : 2 * H])

        w3_raw = keep.tile([P, 2 * H], U8, name="w3_raw", tag="w13", align_bytes=64)
        nc.sync.dma_start(w3_raw[:].bitcast(I32), w3_words[0].bitcast(I32))
        load_scale_rows(on_sync, ws_raw[:, 0:H], w3_scales[0])
        w3 = deal(nc.gpsimd, nc.gpsimd, "w3", w3_raw[:], ws_raw[:, 0:H])
        res_sb = keep.tile([P, PACK, S], F32, name="res_sb", tag="big", align_bytes=64)
        nc.sync.dma_start(res_sb[:], res.rearrange("(p t) s -> p t s", t=PACK))

        y_sb = {}
        c_sb = {}
        for t in Y_ORDER:
            if t == Y_ORDER[0]:
                y_sb[t] = keep.tile([P, S], F32, name=f"y{t}")
                for h in range(2):
                    cols = slice(h * HALF, (h + 1) * HALF)
                    bank = psum.tile([P, HALF], F32, name=f"y_half{h}", tag=f"bank{t + PACK * h}")
                    product(bank[:], w1, t, xa[0][:, cols], xa[1][:, cols])
                    nc.scalar.copy(y_sb[t][:, cols], bank[:])
                continue
            bank = psum.tile([P, S], F32, name=f"y_bank{t}", tag=f"bank{t}")
            product(bank[:], w1, t, xa[0][:], xa[1][:])
            y_t = keep.tile([P, S], F32, name=f"y{t}")
            nc.scalar.copy(y_t[:], bank[:])
            y_sb[t] = y_t
        for t in reversed(range(PACK)):
            bank = psum.tile([P, S], F32, name=f"c_bank{t}", tag=f"bank{PACK + t}")
            product(bank[:], w2, t, xb[0][:], xb[1][:])
            c_t = keep.tile([P, S], F32, name=f"c{t}")
            nc.scalar.activation(c_t[:], bank[:], ACT.Copy, scale=gn_sb[:, t : t + 1])
            c_sb[t] = c_t

        def slot(ring, n, h=None):
            if h is None:
                return ring[:, n * S : (n + 1) * S]
            return ring[:, n * S + h * HALF : n * S + (h + 1) * HALF]

        def entries(offsets, h):
            return offsets[:, h * HALF // 16 : (h + 1) * HALF // 16]

        def fetch_lo(ring, ahead, windows, order):
            for t in order:
                for h in range(S // HALF):
                    nc.vector.tensor_copy(slot(ring, t + ahead, h), windows[t][:].indirect(entries(lo_sb, h)))

        def subtract_from_hi(ring, ahead, windows, t):
            for h in range(S // HALF):
                nc.vector.tensor_tensor(slot(ring, t, h), windows[t][:].indirect(entries(hi_sb, h)), slot(ring, t + ahead, h), ALU.subtract)

        y_ring = keep.tile([P, (2 * PACK + 1) * S], F32, name="y_ring")
        c_ring = keep.tile([P, (PACK + 1) * S], F32, name="c_ring")
        sq = [keep.tile([P, S], F32, name=f"sq{n}", tag=tag, align_bytes=64) for n, tag in enumerate(("xb_words", "w2_words"))]
        root = keep.tile([P, 2 * S], F32, name="root")
        inv = keep.tile([P, PACK * S], F32, name="inv")
        fetch_lo(y_ring, 2, y_sb, Y_ORDER)
        for t in range(PACK):
            subtract_from_hi(y_ring, 2, y_sb, t)
            nc.scalar.activation(sq[t % 2][:], slot(y_ring, t), ACT.Square)
            nc.scalar.activation(slot(root, t % 2), sq[t % 2][:], ACT.Abs_reciprocal_sqrt, bias=0.25)
            nc.scalar.activation(slot(inv, t), slot(root, t % 2), ACT.Square)
        fetch_lo(c_ring, 1, c_sb, C_ORDER)
        for t in range(PACK - 1):
            nc.gpsimd.tensor_tensor(slot(y_ring, PACK + 1 + t), slot(y_ring, t), slot(inv, t), ALU.mult)
        for h in range(2):
            nc.vector.tensor_tensor(slot(y_ring, 2 * PACK, h), slot(y_ring, PACK - 1, h), slot(inv, PACK - 1, h), ALU.mult)
        for t in range(PACK):
            subtract_from_hi(c_ring, 1, c_sb, t)
        slope = y_ring[:, (PACK + 1) * S : (2 * PACK + 1) * S]
        dy = c_ring[:, 0 : PACK * S]

        def by_pairs(rows, j):
            return rows.rearrange("p (t s) -> p t s", t=PACK)[:, :, j * CHUNK : (j + 1) * CHUNK]

        def woven(tile):
            return tile[:].rearrange("p (c t) -> p c t", t=PACK)

        z_words = keep.tile([P, S], U32, name="z_words", align_bytes=64)
        z_scales = keep.tile([P, S], U8, name="z_scales", align_bytes=64)
        o_words = keep.tile([P, S], I32, name="o_words", align_bytes=64)
        o_scales = keep.tile([P, S], U8, name="o_scales", align_bytes=64)
        out_rows = out_0.rearrange("(p t) s -> p t s", t=PACK)
        out_words = out_1[0].rearrange("p c r -> p (c r)").bitcast(I32)
        banks = []
        for j in range(S // CHUNK):
            cols = slice(j * CHUNK, (j + 1) * CHUNK)
            z = keep.tile([P, PACK * CHUNK], BF16, name=f"z{j}", align_bytes=64)
            if j < 2:
                z_rows = keep.tile([P, PACK, CHUNK], BF16, name=f"z_rows{j}")
                nc.vector.tensor_tensor(z_rows[:], by_pairs(slope, j), by_pairs(dy, j), ALU.mult)
                nc.scalar.copy(woven(z), z_rows[:].rearrange("p t c -> p c t"))
            else:
                pairs = "p t (c i) -> p c t i"
                nc.vector.tensor_tensor(z[:].rearrange("p (c i t) -> p c t i", i=2, t=PACK), by_pairs(slope, j).rearrange(pairs, i=2), by_pairs(dy, j).rearrange(pairs, i=2), ALU.mult)
            nc.vector.quantize_mx(out=z_words[:, cols].bitcast(FP8X4), scales=z_scales[:, cols], in_=z[:])
            bank = psum.tile([P, PACK, CHUNK], F32, name=f"o_bank{j}", tag=f"bank{j}")
            for t in range(PACK):
                product(bank[:, t, :], w3, t, z_words[:, cols], z_scales[:, cols])
            banks.append(bank)
        for j in range(S // CHUNK):
            cols = slice(j * CHUNK, (j + 1) * CHUNK)
            o = keep.tile([P, PACK, CHUNK], F32, name=f"o{j}")
            nc.vector.tensor_tensor(o[:], banks[j][:], res_sb[:, :, cols], ALU.add)
            nc.sync.dma_start(out_rows[:, :, cols], o[:])
            ob = keep.tile([P, PACK * CHUNK], BF16, name=f"ob{j}", align_bytes=64)
            nc.scalar.copy(woven(ob), o[:].rearrange("p t c -> p c t"))
            nc.vector.quantize_mx(out=o_words[:, cols].bitcast(FP8X4), scales=o_scales[:, cols], in_=ob[:])
            nc.sync.dma_start(out_words[:, cols], o_words[:, cols])
        for q in range(4):
            (nc.scalar if q % 2 == 0 else nc.sync).dma_start(out_2[0][4 * q : 4 * q + 4, :].bitcast(I32), o_scales[32 * q : 32 * q + 4, :].bitcast(I32))
